import numpy as np
import ml_dtypes


def mxq(x, axis, fmt="e4m3"):
    dtype, down = {"e4m3": (ml_dtypes.float8_e4m3fn, 7), "e5m2": (ml_dtypes.float8_e5m2, 14)}[fmt]
    v = np.moveaxis(np.asarray(x, np.float32).astype(ml_dtypes.bfloat16).astype(np.float64), axis, -1)
    blocks = v.reshape(v.shape[:-1] + (-1, 32))
    amax = np.abs(blocks).max(-1, keepdims=True)
    byte = np.maximum(np.where(amax > 0, np.frexp(amax)[1] - 1 + 127, 0) - down, 1)
    scale = np.exp2(byte - 127.0)
    codes = (blocks / scale).astype(np.float32).astype(dtype).astype(np.float64)
    return np.moveaxis((codes * scale).reshape(v.shape), -1, axis)


WIDE = False


def mx_kscale(k):
    if not WIDE:
        return np.ones(k)
    levels = np.array([10, -10, 5, -5, 0])
    if k % 512:
        return np.exp2(np.random.permutation(np.resize(levels, k // 32))).repeat(32)
    a = np.empty((k // 512, 16))
    for p in range(k // 512):
        a[p, :8] = np.random.permutation(np.resize(levels, 8))
        for g in range(8):
            far = levels[np.abs(levels - a[p, g]) >= 10]
            a[p, g + 8] = far[np.random.randint(len(far))]
    return np.exp2(a.ravel()).repeat(32)


BF16 = ml_dtypes.bfloat16


def bf(x):
    return np.asarray(x, np.float32).astype(BF16)


def f64(x):
    return np.asarray(x).astype(np.float64)

def planes(Y):
    n, m = Y.shape
    b = f64(bf(Y)).reshape(n // 32, 32, m)
    amax = np.abs(b).max(1)
    byte = np.clip(np.where(amax > 0, np.frexp(amax)[1] - 1 + 127 - 7, 1), 1, 254)
    codes = (b * np.exp2(127.0 - byte)[:, None, :]).reshape(n, m).astype(np.float32).astype(ml_dtypes.float8_e4m3fn).view(np.uint8)
    words = codes.reshape(n // 512, 128, 4, m).transpose(0, 1, 3, 2)
    return np.ascontiguousarray(words), np.ascontiguousarray(byte.astype(np.uint8).reshape(n // 512, 16, m))


H, N, E, C, T, EV = 4, 512, 512, 2, 512, 512
M = C * T


def per_source_softmax(s):
    top = np.max(s, axis=-1, keepdims=True)
    w = np.exp(s - top)
    return w / np.sum(w, axis=-1, keepdims=True)


def setup_inputs():
    s, t = mx_kscale(E), mx_kscale(M)
    return {"q": bf(np.random.standard_normal((H, N, E)) * s),
            "k": bf(1.5 * np.random.standard_normal((H, M, E)) / s),
            "v": bf(0.3 * np.random.standard_normal((H, M, EV)) / t[:, None]),
            "g": bf(0.25 * np.sqrt(M) * np.random.standard_normal(M) * t),
            "lam": bf(np.random.uniform(0.3, 1.5, (N, C)))}


def core(q, k, v, g, lam):
    q, k, v, g, lam = f64(q), f64(k), f64(v), f64(g), f64(lam)
    heads, n_pos, width = q.shape
    n_tok = k.shape[1]
    n_src = lam.shape[1]
    per_src = n_tok // n_src

    s = (mxq(q, 2, "e4m3") @ mxq(k, 2, "e4m3").transpose(0, 2, 1)) / np.sqrt(width)

    p = per_source_softmax(s.reshape(heads, n_pos, n_src, per_src))

    r = p * lam[None, :, :, None]

    a = r.reshape(heads, n_pos, n_tok) * g[None, None, :]

    return mxq(a, 2, "e4m3") @ mxq(v, 1, "e4m3")


def reference(q, k, v, g, lam):
    R_out = core(q, k, v, g, lam)
    words, scales = planes(np.moveaxis(R_out, 1, 0).reshape(512, -1))
    return R_out, words, scales

@@ -1,0 +1,391 @@
+from contextlib import ExitStack
+
+import concourse.mybir as mybir
+from concourse.masks import make_identity
+
+H, N, E, C, T, EV = 4, 512, 512, 2, 512, 512
+M = C * T
+FLOPS = 2 * H * N * M * (E + EV)
+
+P = 128
+PACK = 4
+SCALE = 1.0 / E**0.5
+
+F32 = mybir.dt.float32
+BF16 = mybir.dt.bfloat16
+U32 = mybir.dt.uint32
+I32 = mybir.dt.int32
+U8 = mybir.dt.uint8
+FP8X4 = mybir.dt.float8_e4m3fn_x4
+COPY = mybir.ActivationFunctionType.Copy
+EXP = mybir.ActivationFunctionType.Exp
+MULT = mybir.AluOpType.mult
+ADD = mybir.AluOpType.add
+MAX = mybir.AluOpType.max
+AXIS_X = mybir.AxisListType.X
+
+
+def tile_ipadapterregionaldecoupledcrossattention_x1_kernel(tc, q, k, v, g, lam, out, words, scales):
+    nc = tc.nc
+    tiles = H * PACK
+
+    with ExitStack() as ctx:
+        const = ctx.enter_context(tc.tile_pool(name="const", bufs=1))
+        raw = ctx.enter_context(tc.tile_pool(name="raw", bufs=8))
+        grp = ctx.enter_context(tc.tile_pool(name="grp", bufs=3))
+        codes = ctx.enter_context(tc.tile_pool(name="codes", bufs=4))
+        soft = ctx.enter_context(tc.tile_pool(name="soft", bufs=3))
+        res = ctx.enter_context(tc.tile_pool(name="res", bufs=2))
+        psum_g = ctx.enter_context(tc.psum_pool(name="psum_g", bufs=1))
+        psum_s = ctx.enter_context(tc.psum_pool(name="psum_s", bufs=4))
+        psum_w = ctx.enter_context(tc.psum_pool(name="psum_w", bufs=3))
+
+        ctx.enter_context(tc.manual_schedule())
+
+        q_raw, k_raw, v_raw = {}, {}, {}
+
+        def load(store, key, src, tag, bufs, pieces=1, which=None):
+            if key not in store:
+                store[key] = raw.tile([P, PACK, 512], BF16, name=tag, tag=tag, bufs=bufs, align_bytes=64)
+            view = src.rearrange("(p t) e -> p t e", t=PACK)
+            step = PACK // pieces
+            for a in which or range(pieces):
+                part = slice(a * step, (a + 1) * step)
+                nc.sync.dma_start(out=store[key][:, part, :], in_=view[:, part, :])
+
+        def load_k(h, c, halves=1):
+            load(k_raw, (h, c), k[h, c * T : (c + 1) * T, :], "k_raw", 8, halves)
+
+        def load_v(h, c):
+            load(v_raw, (h, c), v[h, c * T : (c + 1) * T, :], "v_raw", 8)
+
+        g_row = const.tile([P, M], BF16, name="g_row")
+        nc.gpsimd.memset(g_row[:], 0.0)
+        lam_raw = const.tile([P, PACK, C], BF16, name="lam_raw")
+        nc.scalar.dma_start(out=lam_raw[:], in_=lam.rearrange("(p t) c -> p t c", t=PACK))
+        nc.scalar.dma_start(out=g_row[0:1, :], in_=g.rearrange("(o m) -> o m", o=1))
+        load(q_raw, 0, q[0], "q_raw", 4, 2, (0,))
+        load_k(0, 0, 2)
+        load_k(0, 1, 2)
+        load(q_raw, 0, q[0], "q_raw", 4, 2, (1,))
+        load(q_raw, 1, q[1], "q_raw", 4)
+        load_v(0, 0)
+        load_v(0, 1)
+        for h in range(1, H):
+            load_k(h, 0)
+            load_k(h, 1)
+            if h + 1 < H:
+                load(q_raw, h + 1, q[h + 1], "q_raw", 4)
+            load_v(h, 0)
+            load_v(h, 1)
+
+        warm = const.tile([P, 1], F32, name="warm")
+        nc.vector.memset(warm[:], 0.0)
+        warm_out = const.tile([P, 1], F32, name="warm_out")
+        nc.scalar.activation(out=warm_out[:], in_=warm[:], func=EXP)
+        ident = const.tile([P, P], F32, name="ident")
+        make_identity(nc, ident[:])
+        ones = const.tile([P, P], BF16, name="ones")
+        nc.vector.memset(ones[:], 1.0)
+        lam_f = const.tile([P, PACK, C], F32, name="lam_f")
+        g_turned = const.tile([P, M], BF16, name="g_turned")
+        gain = psum_g.tile([P, C, T], BF16, name="gain")
+
+        def make_gain():
+            nc.vector.tensor_copy(
+                out=g_turned[:].rearrange("o (c u p e) -> o c u p e", c=C, u=2, e=2),
+                in_=g_row[:].rearrange("o (c p u e) -> o c u p e", c=C, u=2, e=2),
+            )
+            nc.vector.tensor_copy(out=lam_f[:], in_=lam_raw[:])
+            for c in range(C):
+                nc.tensor.matmul(gain[:, c, :], lhsT=ones[:], rhs=g_turned[:, c * T : (c + 1) * T], start=True, stop=True)
+
+        grouped, qc, kc, vc = {}, {}, {}, {}
+
+        def copy_on(engine, out_ap, in_ap):
+            if engine == "V":
+                nc.vector.tensor_copy(out=out_ap, in_=in_ap)
+            else:
+                nc.scalar.copy(out=out_ap, in_=in_ap)
+
+        turned = {}
+
+        def turn_only(key, b):
+            src = q_raw[key[0]] if len(key) == 1 else k_raw[key]
+            bank = psum_w.tile([P, 2, 2, P], F32, name="w_ps")
+            word = src[:].rearrange("p t e -> p (t e)").bitcast(F32).rearrange("p (t e) -> p t e", t=PACK)
+            for s in range(2):
+                for u in range(2):
+                    nc.tensor.transpose(bank[:, s, u, :], word[:, 2 * b + s, u::2], ident[:])
+            turned[key, b] = bank
+
+        def copy_turn(key, b, engine):
+            bank = turned.pop((key, b))
+            if b == 0:
+                grouped[key] = grp.tile([P, 512, PACK], BF16, name="qk_grp", tag="qk_grp", bufs=4, align_bytes=64)
+            dst = grouped[key][:].rearrange("p n j -> p (n j)").bitcast(F32)[:, 512 * b : 512 * (b + 1)]
+            if len(key) == 1:
+                copy_on(engine, dst.rearrange("p (s n u) -> p s n u", s=2, u=2), bank[:].rearrange("p s u n -> p s n u"))
+            else:
+                copy_on(engine, dst.rearrange("p (n s u) -> p n s u", s=2, u=2), bank[:].rearrange("p s u n -> p n s u"))
+
+        def turn(key, b, engine):
+            turn_only(key, b)
+            copy_turn(key, b, engine)
+
+        def quant(src, tag, bufs, parts=1, made=None, which=None):
+            if made is None:
+                cod = codes.tile([P, 512], U32, name=tag, tag=tag, bufs=bufs, align_bytes=64)
+                sca = codes.tile([P, 512], U8, name=tag + "_s", tag=tag + "_s", bufs=bufs, align_bytes=64)
+            else:
+                cod, sca = made
+            width = 512 // parts
+            for a in which or range(parts):
+                cols = slice(a * width, (a + 1) * width)
+                nc.vector.quantize_mx(out=cod[:, cols].bitcast(FP8X4), scales=sca[:, cols], in_=src[:, cols, :].rearrange("p n j -> p (n j)"))
+            return cod, sca
+
+        def quant_q(h):
+            qc[h] = quant(grouped.pop((h,)), "q_cod", 2)
+
+        def quant_k(h, c):
+            kc[h, c] = quant(grouped.pop((h, c)), "k_cod", 4)
+
+        v_grp = {}
+
+        def weave(dst, src, engine, lo, hi):
+            cols = slice(lo, hi)
+            dst = dst[:, cols, :].rearrange("p (w i) j -> p w j i", i=4)
+            src = src[:, :, cols].rearrange("p j (w i) -> p w j i", i=4)
+            if engine == "G":
+                nc.gpsimd.tensor_scalar(out=dst, in0=src, scalar1=1.0, scalar2=0.0, op0=MULT, op1=ADD)
+            else:
+                copy_on(engine, dst, src)
+
+        def weave_v(h, c, engine, lo=0, hi=EV):
+            if (h, c) not in v_grp:
+                v_grp[h, c] = grp.tile([P, EV, PACK], BF16, name="v_grp", tag="v_grp", bufs=3, align_bytes=64)
+            weave(v_grp[h, c], v_raw[h, c], engine, lo, hi)
+
+        def quant_v(h, c):
+            vc[h, c] = quant(v_grp.pop((h, c)), "v_cod", 4)
+
+        s_ps, stat, expo, a_bf, a_ps, a_grp, a_cod, o_ps = {}, {}, {}, {}, {}, {}, {}, {}
+        o_sb, o_grp = {}, {}
+
+        def score(i, c):
+            h, t = divmod(i, PACK)
+            if c == 0:
+                for n in range(C):
+                    s_ps[i, n] = psum_s.tile([P, T], F32, name="s_ps")
+            bank = s_ps[i, c]
+            cols = slice(t * P, (t + 1) * P)
+            nc.tensor.matmul_mx(
+                out=bank[:],
+                lhsT=qc[h][0][:, cols].bitcast(FP8X4),
+                lhsT_scale=qc[h][1][:, cols],
+                rhs=kc[h, c][0][:].bitcast(FP8X4),
+                rhs_scale=kc[h, c][1][:],
+                start=True,
+                stop=True,
+            )
+
+        def top(i, c):
+            if c == 0:
+                stat[i] = soft.tile([P, 40], F32, name="stat", tag="stat", bufs=4)
+            nc.vector.tensor_reduce(out=stat[i][:, c : c + 1], in_=s_ps[i, c][:], axis=AXIS_X, op=MAX)
+
+        def shift(i):
+            st = stat[i]
+            nc.scalar.activation(out=st[:, 8:10], in_=st[:, 0:2], func=COPY, scale=-SCALE)
+
+        def expon(i, c):
+            if c == 0:
+                expo[i] = soft.tile([P, C, T], F32, name="expo", tag="expo", bufs=3)
+            st = stat[i]
+            nc.scalar.activation(
+                out=expo[i][:, c, :], in_=s_ps.pop((i, c))[:], func=EXP, bias=st[:, 8 + c : 9 + c], scale=SCALE, accum_out=st[:, 16 + c : 17 + c]
+            )
+
+        def recip(i):
+            st = stat[i]
+            nc.vector.reciprocal(out=st[:, 24:26], in_=st[:, 16:18])
+
+        def factor(i):
+            st = stat[i]
+            nc.gpsimd.tensor_tensor(out=st[:, 32:34], in0=st[:, 24:26], in1=lam_f[:, i % PACK, :], op=MULT)
+
+        def weigh(i, c):
+            if c == 0:
+                a_bf[i] = soft.tile([P, C, T], BF16, name="a_bf", tag="a_bf", bufs=3, align_bytes=64)
+            nc.vector.scalar_tensor_tensor(
+                out=a_bf[i][:, c, :], in0=expo[i][:, c, :], scalar=stat[i][:, 32 + c : 33 + c], in1=gain[:, c, :], op0=MULT, op1=MULT
+            )
+
+        def turn_a(i, c):
+            if c == 0:
+                a_ps[i] = psum_w.tile([P, 2, 2, P], F32, name="w_ps")
+            word = a_bf[i][:, c, :].bitcast(F32)
+            for u in range(2):
+                nc.tensor.transpose(a_ps[i][:, c, u, :], word[:, u * P : (u + 1) * P], ident[:])
+
+        def copy_a(i, engine):
+            a_grp[i] = soft.tile([P, C, P, PACK], BF16, name="a_grp", tag="a_grp", bufs=3, align_bytes=64)
+            dst = a_grp[i][:].rearrange("p c n j -> p (c n j)").bitcast(F32).rearrange("p (c n u) -> p c n u", c=C, u=2)
+            bank = a_ps.pop(i)[:].rearrange("p c u n -> p c n u")
+            if engine == "VS":
+                copy_on("S", dst[:, 0], bank[:, 0])
+                copy_on("V", dst[:, 1], bank[:, 1])
+            else:
+                copy_on(engine, dst, bank)
+
+        def quant_a(i):
+            cod = soft.tile([P, C * P], U32, name="a_cod", tag="a_cod", bufs=3, align_bytes=64)
+            sca = soft.tile([P, C * P], U8, name="a_sca", tag="a_sca", bufs=3, align_bytes=64)
+            nc.vector.quantize_mx(out=cod[:].bitcast(FP8X4), scales=sca[:], in_=a_grp.pop(i)[:].rearrange("p c n j -> p (c n j)"))
+            a_cod[i] = (cod, sca)
+
+        def mix(i):
+            h = i // PACK
+            bank = psum_w.tile([P, EV], F32, name="w_ps")
+            cod, sca = a_cod.pop(i)
+            for c in range(C):
+                cols = slice(c * P, (c + 1) * P)
+                nc.tensor.matmul_mx(
+                    out=bank[:],
+                    lhsT=cod[:, cols].bitcast(FP8X4),
+                    lhsT_scale=sca[:, cols],
+                    rhs=vc[h, c][0][:].bitcast(FP8X4),
+                    rhs_scale=vc[h, c][1][:],
+                    start=(c == 0),
+                    stop=(c == C - 1),
+                )
+            o_ps[i] = bank
+
+        def copy_o(i, split=EV):
+            h, t = divmod(i, PACK)
+            if t == 0:
+                o_sb[h] = res.tile([P, PACK, EV], F32, name="o_sb", tag="o_sb", bufs=3)
+            bank = o_ps.pop(i)
+            nc.scalar.copy(out=o_sb[h][:, t, :split], in_=bank[:, :split])
+            if split < EV:
+                nc.vector.tensor_copy(out=o_sb[h][:, t, split:], in_=bank[:, split:])
+
+        def store_o(h, lo, hi):
+            nc.sync.dma_start(out=out[h].rearrange("(p t) e -> p t e", t=PACK)[:, lo:hi, :], in_=o_sb[h][:, lo:hi, :])
+
+        def weave_o(h, engine, lo=0, hi=EV):
+            if h not in o_grp:
+                o_grp[h] = res.tile([P, EV, PACK], BF16, name="o_grp", tag="o_grp", bufs=2, align_bytes=64)
+            weave(o_grp[h], o_sb[h], engine, lo, hi)
+
+        def planes(h, parts=1):
+            cod, sca = quant(o_grp[h], "p_cod", 2, parts)
+            width = EV // parts
+            for a in range(parts):
+                cols = slice(h * EV + a * width, h * EV + (a + 1) * width)
+                here = slice(a * width, (a + 1) * width)
+                nc.sync.dma_start(out=words[0, :, cols, :].rearrange("p m t -> p (m t)").bitcast(I32), in_=cod[:, here].bitcast(I32))
+            cols = slice(h * EV, (h + 1) * EV)
+            for b in range(4):
+                nc.sync.dma_start(out=scales[0, 4 * b : 4 * b + 4, cols].bitcast(I32), in_=sca[32 * b : 32 * b + 4, :].bitcast(I32))
+
+        OW = 384
+
+        def prep(n):
+            h, t = divmod(n + 1, PACK)
+            return None if t == 3 or h + 1 >= H else ((h + 1,), (h + 1, 0), (h + 1, 1))[t]
+
+        turn((0,), 0, "V")
+        turn((0, 0), 0, "S")
+        qc[0] = quant(grouped[0,], "q_cod", 2, 2, None, (0,))
+        turn((0, 0), 1, "V")
+        turn((0, 1), 0, "S")
+        quant_k(0, 0)
+        turn((0, 1), 1, "S")
+        score(0, 0)
+        turn((0,), 1, "S")
+        top(0, 0)
+        quant_k(0, 1)
+        score(0, 1)
+        score(1, 0)
+        score(1, 1)
+        make_gain()
+        top(0, 1)
+        shift(0)
+        expon(0, 0)
+        expon(0, 1)
+        quant(grouped.pop((0,)), "q_cod", 2, 2, qc[0], (1,))
+        turn(prep(-1), 0, "V")
+        turn(prep(-1), 1, "S")
+        weave_v(0, 0, "V")
+
+        for i in range(tiles + 2):
+            h, t = divmod(i, PACK)
+            live = i < tiles
+            more = h + 1 < H
+            if 2 <= i <= tiles:
+                quant_a(i - 2)
+            if live:
+                if t == 0:
+                    quant_v(h, 0)
+                if t == 1 and more:
+                    quant_q(h + 1)
+                    quant_k(h + 1, 0)
+                if t == 2:
+                    quant_v(h, 1)
+                    if more:
+                        quant_k(h + 1, 1)
+            if live:
+                recip(i)
+                factor(i)
+                if t < 2:
+                    weave_v(h, 1, "G", 256 * t, 256 * t + 256)
+                elif more:
+                    weave_v(h + 1, 0, "G", 256 * (t - 2), 256 * (t - 2) + 256)
+            key = prep(i) if live else None
+            if key:
+                turn_only(key, 0)
+                turn_only(key, 1)
+            if 1 <= i <= tiles:
+                copy_a(i - 1, "S" if live else "VS")
+            if key:
+                copy_turn(key, 0, "S")
+                copy_turn(key, 1, "S")
+            if i + 2 < tiles:
+                score(i + 2, 0)
+                score(i + 2, 1)
+            if 2 <= i <= tiles:
+                mix(i - 2)
+            if i == tiles:
+                quant_a(i - 1)
+                mix(i - 1)
+            if i + 1 < tiles:
+                top(i + 1, 0)
+                top(i + 1, 1)
+                shift(i + 1)
+                expon(i + 1, 0)
+                expon(i + 1, 1)
+            if 2 <= i <= tiles:
+                copy_o(i - 2)
+                if (i - 2) % PACK == 3:
+                    store_o((i - 2) // PACK, 0, 4)
+                if i == tiles:
+                    store_o(H - 1, 0, 3)
+            if live and h > 0 and t == 2:
+                weave_o(h - 1, "S", 0, OW)
+            if live:
+                weigh(i, 0)
+                turn_a(i, 0)
+                weigh(i, 1)
+                turn_a(i, 1)
+            if live and h > 0 and t == 3:
+                weave_o(h - 1, "V", OW, EV)
+                planes(h - 1)
+
+        hl = H - 1
+        copy_o(tiles - 1, EV // 2)
+        store_o(hl, 3, 4)
+        weave_o(hl, "V", 0, 256)
+        weave_o(hl, "V", 256, 512)
+        planes(hl, 2)

@@ -69,15 +69,18 @@ def tile_ipadapterregionaldecoupledcrossattention_x1_kernel(tc, q, k, v, g, lam,
         load_k(0, 1, 2)
         load(q_raw, 0, q[0], "q_raw", 4, 2, (1,))
         load(q_raw, 1, q[1], "q_raw", 4)
+        load_k(1, 0)
         load_v(0, 0)
+        load_k(1, 1)
         load_v(0, 1)
-        for h in range(1, H):
+        for h in range(2, H):
+            load(q_raw, h, q[h], "q_raw", 4)
             load_k(h, 0)
+            load_v(h - 1, 0)
             load_k(h, 1)
-            if h + 1 < H:
-                load(q_raw, h + 1, q[h + 1], "q_raw", 4)
-            load_v(h, 0)
-            load_v(h, 1)
+            load_v(h - 1, 1)
+        load_v(H - 1, 0)
+        load_v(H - 1, 1)
 
         warm = const.tile([P, 1], F32, name="warm")
         nc.vector.memset(warm[:], 0.0)
@@ -89,14 +92,16 @@ def tile_ipadapterregionaldecoupledcrossattention_x1_kernel(tc, q, k, v, g, lam,
         nc.vector.memset(ones[:], 1.0)
         lam_f = const.tile([P, PACK, C], F32, name="lam_f")
         g_turned = const.tile([P, M], BF16, name="g_turned")
+        nc.gpsimd.tensor_copy(
+            out=g_turned[:].rearrange("o (c u p e) -> o c u p e", c=C, u=2, e=2),
+            in_=g_row[:].rearrange("o (c p u e) -> o c u p e", c=C, u=2, e=2),
+        )
+        nc.gpsimd.tensor_copy(out=lam_f[:], in_=lam_raw[:])
         gain = psum_g.tile([P, C, T], BF16, name="gain")
 
+        gain_sb = const.tile([P, T], BF16, name="gain_sb")
+
         def make_gain():
-            nc.vector.tensor_copy(
-                out=g_turned[:].rearrange("o (c u p e) -> o c u p e", c=C, u=2, e=2),
-                in_=g_row[:].rearrange("o (c p u e) -> o c u p e", c=C, u=2, e=2),
-            )
-            nc.vector.tensor_copy(out=lam_f[:], in_=lam_raw[:])
             for c in range(C):
                 nc.tensor.matmul(gain[:, c, :], lhsT=ones[:], rhs=g_turned[:, c * T : (c + 1) * T], start=True, stop=True)
 
@@ -211,9 +216,9 @@ def tile_ipadapterregionaldecoupledcrossattention_x1_kernel(tc, q, k, v, g, lam,
             st = stat[i]
             nc.vector.reciprocal(out=st[:, 24:26], in_=st[:, 16:18])
 
-        def factor(i):
+        def factor(i, eng=None):
             st = stat[i]
-            nc.gpsimd.tensor_tensor(out=st[:, 32:34], in0=st[:, 24:26], in1=lam_f[:, i % PACK, :], op=MULT)
+            (eng or nc.gpsimd).tensor_tensor(out=st[:, 32:34], in0=st[:, 24:26], in1=lam_f[:, i % PACK, :], op=MULT)
 
         def weigh(i, c):
             if c == 0:
@@ -221,6 +226,15 @@ def tile_ipadapterregionaldecoupledcrossattention_x1_kernel(tc, q, k, v, g, lam,
             nc.vector.scalar_tensor_tensor(
                 out=a_bf[i][:, c, :], in0=expo[i][:, c, :], scalar=stat[i][:, 32 + c : 33 + c], in1=gain[:, c, :], op0=MULT, op1=MULT
             )
+
+        half = {}
+
+        def gain_on_gpsimd(i):
+            half[i] = soft.tile([P, T], F32, name="half", tag="half", bufs=2)
+            nc.gpsimd.tensor_tensor(out=half[i][:], in0=expo[i][:, 1, :], in1=gain_sb[:], op=MULT)
+
+        def factor_on_scalar(i):
+            nc.scalar.activation(out=a_bf[i][:, 1, :], in_=half.pop(i)[:], func=COPY, scale=stat[i][:, 33:34])
 
         def turn_a(i, c):
             if c == 0:
@@ -239,10 +253,14 @@ def tile_ipadapterregionaldecoupledcrossattention_x1_kernel(tc, q, k, v, g, lam,
             else:
                 copy_on(engine, dst, bank)
 
-        def quant_a(i):
+        def quant_a(i, parts=1):
             cod = soft.tile([P, C * P], U32, name="a_cod", tag="a_cod", bufs=3, align_bytes=64)
             sca = soft.tile([P, C * P], U8, name="a_sca", tag="a_sca", bufs=3, align_bytes=64)
-            nc.vector.quantize_mx(out=cod[:].bitcast(FP8X4), scales=sca[:], in_=a_grp.pop(i)[:].rearrange("p c n j -> p (c n j)"))
+            src = a_grp.pop(i)[:].rearrange("p c n j -> p (c n j)")
+            width = C * P // parts
+            for n in range(parts):
+                cols = slice(n * width, (n + 1) * width)
+                nc.vector.quantize_mx(out=cod[:, cols].bitcast(FP8X4), scales=sca[:, cols], in_=src[:, PACK * n * width : PACK * (n + 1) * width])
             a_cod[i] = (cod, sca)
 
         def mix(i):
@@ -291,9 +309,11 @@ def tile_ipadapterregionaldecoupledcrossattention_x1_kernel(tc, q, k, v, g, lam,
                 nc.sync.dma_start(out=scales[0, 4 * b : 4 * b + 4, cols].bitcast(I32), in_=sca[32 * b : 32 * b + 4, :].bitcast(I32))
 
         OW = 384
+        OFF = ()
+        PIECES = ((1, 0, 0, 256), (1, 1, 256, 512), (0, 2, 0, 256), (0, 3, 256, 512))
 
         def prep(n):
-            h, t = divmod(n + 1, PACK)
+            h, t = divmod(n + 2, PACK)
             return None if t == 3 or h + 1 >= H else ((h + 1,), (h + 1, 0), (h + 1, 1))[t]
 
         turn((0,), 0, "V")
@@ -304,88 +324,118 @@ def tile_ipadapterregionaldecoupledcrossattention_x1_kernel(tc, q, k, v, g, lam,
         quant_k(0, 0)
         turn((0, 1), 1, "S")
         score(0, 0)
+        score(1, 0)
         turn((0,), 1, "S")
         top(0, 0)
         quant_k(0, 1)
+        top(1, 0)
+        turn(prep(-2), 0, "S")
         score(0, 1)
-        score(1, 0)
         score(1, 1)
         make_gain()
         top(0, 1)
         shift(0)
+        turn_only(prep(-2), 1)
+        top(1, 1)
         expon(0, 0)
         expon(0, 1)
+        shift(1)
         quant(grouped.pop((0,)), "q_cod", 2, 2, qc[0], (1,))
-        turn(prep(-1), 0, "V")
+        copy_turn(prep(-2), 1, "S")
+        weave_v(0, 0, "V", 0, 512)
+        quant_q(1)
+        turn(prep(-1), 0, "S")
+        score(2, 0)
+        score(2, 1)
         turn(prep(-1), 1, "S")
-        weave_v(0, 0, "V")
 
-        for i in range(tiles + 2):
+        for i in range(tiles - 1):
             h, t = divmod(i, PACK)
-            live = i < tiles
             more = h + 1 < H
-            if 2 <= i <= tiles:
+            if i >= 2:
                 quant_a(i - 2)
-            if live:
-                if t == 0:
-                    quant_v(h, 0)
-                if t == 1 and more:
-                    quant_q(h + 1)
-                    quant_k(h + 1, 0)
-                if t == 2:
-                    quant_v(h, 1)
-                    if more:
-                        quant_k(h + 1, 1)
-            if live:
-                recip(i)
-                factor(i)
-                if t < 2:
-                    weave_v(h, 1, "G", 256 * t, 256 * t + 256)
-                elif more:
-                    weave_v(h + 1, 0, "G", 256 * (t - 2), 256 * (t - 2) + 256)
-            key = prep(i) if live else None
+            if t == 0 and more:
+                quant_k(h + 1, 0)
+            if t == 1:
+                quant_v(h, 0)
+                if more:
+                    quant_k(h + 1, 1)
+            if t == 2:
+                quant_v(h, 1)
+            if t == 3 and h + 2 < H:
+                quant_q(h + 2)
+            recip(i)
+            factor(i)
+            offload = t in OFF
+            if offload:
+                gain_on_gpsimd(i)
+            for part, t0, lo, hi in PIECES:
+                if t0 == t and h + (part == 0) < H:
+                    weave_v(h + (part == 0), part, "G", lo, hi)
+            expon(i + 1, 0)
+            expon(i + 1, 1)
+            if i == 0:
+                nc.scalar.copy(out=gain_sb[:], in_=gain[:, 1, :])
+            key = prep(i)
             if key:
                 turn_only(key, 0)
                 turn_only(key, 1)
-            if 1 <= i <= tiles:
-                copy_a(i - 1, "S" if live else "VS")
+            if i >= 1:
+                copy_a(i - 1, "S")
             if key:
                 copy_turn(key, 0, "S")
                 copy_turn(key, 1, "S")
-            if i + 2 < tiles:
-                score(i + 2, 0)
-                score(i + 2, 1)
-            if 2 <= i <= tiles:
+            if i >= 2:
                 mix(i - 2)
-            if i == tiles:
-                quant_a(i - 1)
-                mix(i - 1)
-            if i + 1 < tiles:
-                top(i + 1, 0)
-                top(i + 1, 1)
-                shift(i + 1)
-                expon(i + 1, 0)
-                expon(i + 1, 1)
-            if 2 <= i <= tiles:
+            if i + 3 < tiles:
+                score(i + 3, 0)
+                score(i + 3, 1)
+            if i + 2 < tiles:
+                top(i + 2, 0)
+                top(i + 2, 1)
+            weigh(i, 0)
+            turn_a(i, 0)
+            if offload:
+                factor_on_scalar(i)
+            else:
+                weigh(i, 1)
+            if i + 2 < tiles:
+                shift(i + 2)
+            turn_a(i, 1)
+            if i >= 2:
                 copy_o(i - 2)
                 if (i - 2) % PACK == 3:
                     store_o((i - 2) // PACK, 0, 4)
-                if i == tiles:
-                    store_o(H - 1, 0, 3)
-            if live and h > 0 and t == 2:
+                elif h == H - 1 and t >= 2:
+                    store_o(h, t - 2, t - 1)
+            if h > 0 and t == 1:
                 weave_o(h - 1, "S", 0, OW)
-            if live:
-                weigh(i, 0)
-                turn_a(i, 0)
-                weigh(i, 1)
-                turn_a(i, 1)
-            if live and h > 0 and t == 3:
-                weave_o(h - 1, "V", OW, EV)
+            if h > 0 and t == 2:
+                if OW < EV:
+                    weave_o(h - 1, "V", OW, EV)
                 planes(h - 1)
 
-        hl = H - 1
-        copy_o(tiles - 1, EV // 2)
-        store_o(hl, 3, 4)
-        weave_o(hl, "V", 0, 256)
-        weave_o(hl, "V", 256, 512)
-        planes(hl, 2)
+        z = tiles - 1
+        quant_a(z - 2)
+        recip(z)
+        factor(z, nc.vector)
+        copy_a(z - 1, "S")
+        mix(z - 2)
+        weigh(z, 0)
+        turn_a(z, 0)
+        copy_o(z - 2)
+        store_o(H - 1, 1, 2)
+        weigh(z, 1)
+        turn_a(z, 1)
+        quant_a(z - 1)
+        copy_a(z, "VS")
+        mix(z - 1)
+        quant_a(z, 2)
+        copy_o(z - 1)
+        store_o(H - 1, 2, 3)
+        mix(z)
+        copy_o(z, EV // 2)
+        store_o(H - 1, 3, 4)
+        weave_o(H - 1, "V", 0, 256)
+        weave_o(H - 1, "V", 256, 512)
+        planes(H - 1, 2)

from contextlib import ExitStack

import concourse.mybir as mybir
from concourse.masks import make_identity

H, N, E, C, T, EV = 4, 512, 512, 2, 512, 512
M = C * T
FLOPS = 2 * H * N * M * (E + EV)

P = 128
PACK = 4
SCALE = 1.0 / E**0.5

F32 = mybir.dt.float32
BF16 = mybir.dt.bfloat16
U32 = mybir.dt.uint32
I32 = mybir.dt.int32
U8 = mybir.dt.uint8
FP8X4 = mybir.dt.float8_e4m3fn_x4
COPY = mybir.ActivationFunctionType.Copy
EXP = mybir.ActivationFunctionType.Exp
MULT = mybir.AluOpType.mult
ADD = mybir.AluOpType.add
MAX = mybir.AluOpType.max
AXIS_X = mybir.AxisListType.X


def tile_ipadapterregionaldecoupledcrossattention_x1_kernel(tc, q, k, v, g, lam, out, words, scales):
    nc = tc.nc
    tiles = H * PACK

    with ExitStack() as ctx:
        const = ctx.enter_context(tc.tile_pool(name="const", bufs=1))
        raw = ctx.enter_context(tc.tile_pool(name="raw", bufs=8))
        grp = ctx.enter_context(tc.tile_pool(name="grp", bufs=3))
        codes = ctx.enter_context(tc.tile_pool(name="codes", bufs=4))
        soft = ctx.enter_context(tc.tile_pool(name="soft", bufs=3))
        res = ctx.enter_context(tc.tile_pool(name="res", bufs=2))
        psum_g = ctx.enter_context(tc.psum_pool(name="psum_g", bufs=1))
        psum_s = ctx.enter_context(tc.psum_pool(name="psum_s", bufs=4))
        psum_w = ctx.enter_context(tc.psum_pool(name="psum_w", bufs=3))

        ctx.enter_context(tc.manual_schedule())

        q_raw, k_raw, v_raw = {}, {}, {}

        def load(store, key, src, tag, bufs, pieces=1, which=None):
            if key not in store:
                store[key] = raw.tile([P, PACK, 512], BF16, name=tag, tag=tag, bufs=bufs, align_bytes=64)
            view = src.rearrange("(p t) e -> p t e", t=PACK)
            step = PACK // pieces
            for a in which or range(pieces):
                part = slice(a * step, (a + 1) * step)
                nc.sync.dma_start(out=store[key][:, part, :], in_=view[:, part, :])

        def load_k(h, c, halves=1):
            load(k_raw, (h, c), k[h, c * T : (c + 1) * T, :], "k_raw", 8, halves)

        def load_v(h, c):
            load(v_raw, (h, c), v[h, c * T : (c + 1) * T, :], "v_raw", 8)

        g_row = const.tile([P, M], BF16, name="g_row")
        nc.gpsimd.memset(g_row[:], 0.0)
        lam_raw = const.tile([P, PACK, C], BF16, name="lam_raw")
        nc.scalar.dma_start(out=lam_raw[:], in_=lam.rearrange("(p t) c -> p t c", t=PACK))
        nc.scalar.dma_start(out=g_row[0:1, :], in_=g.rearrange("(o m) -> o m", o=1))
        load(q_raw, 0, q[0], "q_raw", 4, 2, (0,))
        load_k(0, 0, 2)
        load_k(0, 1, 2)
        load(q_raw, 0, q[0], "q_raw", 4, 2, (1,))
        load(q_raw, 1, q[1], "q_raw", 4)
        load_k(1, 0)
        load_v(0, 0)
        load_k(1, 1)
        load_v(0, 1)
        for h in range(2, H):
            load(q_raw, h, q[h], "q_raw", 4)
            load_k(h, 0)
            load_v(h - 1, 0)
            load_k(h, 1)
            load_v(h - 1, 1)
        load_v(H - 1, 0)
        load_v(H - 1, 1)

        warm = const.tile([P, 1], F32, name="warm")
        nc.vector.memset(warm[:], 0.0)
        warm_out = const.tile([P, 1], F32, name="warm_out")
        nc.scalar.activation(out=warm_out[:], in_=warm[:], func=EXP)
        ident = const.tile([P, P], F32, name="ident")
        make_identity(nc, ident[:])
        ones = const.tile([P, P], BF16, name="ones")
        nc.vector.memset(ones[:], 1.0)
        lam_f = const.tile([P, PACK, C], F32, name="lam_f")
        g_turned = const.tile([P, M], BF16, name="g_turned")
        nc.gpsimd.tensor_copy(
            out=g_turned[:].rearrange("o (c u p e) -> o c u p e", c=C, u=2, e=2),
            in_=g_row[:].rearrange("o (c p u e) -> o c u p e", c=C, u=2, e=2),
        )
        nc.gpsimd.tensor_copy(out=lam_f[:], in_=lam_raw[:])
        gain = psum_g.tile([P, C, T], BF16, name="gain")

        gain_sb = const.tile([P, T], BF16, name="gain_sb")

        def make_gain():
            for c in range(C):
                nc.tensor.matmul(gain[:, c, :], lhsT=ones[:], rhs=g_turned[:, c * T : (c + 1) * T], start=True, stop=True)

        grouped, qc, kc, vc = {}, {}, {}, {}

        def copy_on(engine, out_ap, in_ap):
            if engine == "V":
                nc.vector.tensor_copy(out=out_ap, in_=in_ap)
            else:
                nc.scalar.copy(out=out_ap, in_=in_ap)

        turned = {}

        def turn_only(key, b):
            src = q_raw[key[0]] if len(key) == 1 else k_raw[key]
            bank = psum_w.tile([P, 2, 2, P], F32, name="w_ps")
            word = src[:].rearrange("p t e -> p (t e)").bitcast(F32).rearrange("p (t e) -> p t e", t=PACK)
            for s in range(2):
                for u in range(2):
                    nc.tensor.transpose(bank[:, s, u, :], word[:, 2 * b + s, u::2], ident[:])
            turned[key, b] = bank

        def copy_turn(key, b, engine):
            bank = turned.pop((key, b))
            if b == 0:
                grouped[key] = grp.tile([P, 512, PACK], BF16, name="qk_grp", tag="qk_grp", bufs=4, align_bytes=64)
            dst = grouped[key][:].rearrange("p n j -> p (n j)").bitcast(F32)[:, 512 * b : 512 * (b + 1)]
            if len(key) == 1:
                copy_on(engine, dst.rearrange("p (s n u) -> p s n u", s=2, u=2), bank[:].rearrange("p s u n -> p s n u"))
            else:
                copy_on(engine, dst.rearrange("p (n s u) -> p n s u", s=2, u=2), bank[:].rearrange("p s u n -> p n s u"))

        def turn(key, b, engine):
            turn_only(key, b)
            copy_turn(key, b, engine)

        def quant(src, tag, bufs, parts=1, made=None, which=None):
            if made is None:
                cod = codes.tile([P, 512], U32, name=tag, tag=tag, bufs=bufs, align_bytes=64)
                sca = codes.tile([P, 512], U8, name=tag + "_s", tag=tag + "_s", bufs=bufs, align_bytes=64)
            else:
                cod, sca = made
            width = 512 // parts
            for a in which or range(parts):
                cols = slice(a * width, (a + 1) * width)
                nc.vector.quantize_mx(out=cod[:, cols].bitcast(FP8X4), scales=sca[:, cols], in_=src[:, cols, :].rearrange("p n j -> p (n j)"))
            return cod, sca

        def quant_q(h):
            qc[h] = quant(grouped.pop((h,)), "q_cod", 2)

        def quant_k(h, c):
            kc[h, c] = quant(grouped.pop((h, c)), "k_cod", 4)

        v_grp = {}

        def weave(dst, src, engine, lo, hi):
            cols = slice(lo, hi)
            dst = dst[:, cols, :].rearrange("p (w i) j -> p w j i", i=4)
            src = src[:, :, cols].rearrange("p j (w i) -> p w j i", i=4)
            if engine == "G":
                nc.gpsimd.tensor_scalar(out=dst, in0=src, scalar1=1.0, scalar2=0.0, op0=MULT, op1=ADD)
            else:
                copy_on(engine, dst, src)

        def weave_v(h, c, engine, lo=0, hi=EV):
            if (h, c) not in v_grp:
                v_grp[h, c] = grp.tile([P, EV, PACK], BF16, name="v_grp", tag="v_grp", bufs=3, align_bytes=64)
            weave(v_grp[h, c], v_raw[h, c], engine, lo, hi)

        def quant_v(h, c):
            vc[h, c] = quant(v_grp.pop((h, c)), "v_cod", 4)

        s_ps, stat, expo, a_bf, a_ps, a_grp, a_cod, o_ps = {}, {}, {}, {}, {}, {}, {}, {}
        o_sb, o_grp = {}, {}

        def score(i, c):
            h, t = divmod(i, PACK)
            if c == 0:
                for n in range(C):
                    s_ps[i, n] = psum_s.tile([P, T], F32, name="s_ps")
            bank = s_ps[i, c]
            cols = slice(t * P, (t + 1) * P)
            nc.tensor.matmul_mx(
                out=bank[:],
                lhsT=qc[h][0][:, cols].bitcast(FP8X4),
                lhsT_scale=qc[h][1][:, cols],
                rhs=kc[h, c][0][:].bitcast(FP8X4),
                rhs_scale=kc[h, c][1][:],
                start=True,
                stop=True,
            )

        def top(i, c):
            if c == 0:
                stat[i] = soft.tile([P, 40], F32, name="stat", tag="stat", bufs=4)
            nc.vector.tensor_reduce(out=stat[i][:, c : c + 1], in_=s_ps[i, c][:], axis=AXIS_X, op=MAX)

        def shift(i):
            st = stat[i]
            nc.scalar.activation(out=st[:, 8:10], in_=st[:, 0:2], func=COPY, scale=-SCALE)

        def expon(i, c):
            if c == 0:
                expo[i] = soft.tile([P, C, T], F32, name="expo", tag="expo", bufs=3)
            st = stat[i]
            nc.scalar.activation(
                out=expo[i][:, c, :], in_=s_ps.pop((i, c))[:], func=EXP, bias=st[:, 8 + c : 9 + c], scale=SCALE, accum_out=st[:, 16 + c : 17 + c]
            )

        def recip(i):
            st = stat[i]
            nc.vector.reciprocal(out=st[:, 24:26], in_=st[:, 16:18])

        def factor(i, eng=None):
            st = stat[i]
            (eng or nc.gpsimd).tensor_tensor(out=st[:, 32:34], in0=st[:, 24:26], in1=lam_f[:, i % PACK, :], op=MULT)

        def weigh(i, c):
            if c == 0:
                a_bf[i] = soft.tile([P, C, T], BF16, name="a_bf", tag="a_bf", bufs=3, align_bytes=64)
            nc.vector.scalar_tensor_tensor(
                out=a_bf[i][:, c, :], in0=expo[i][:, c, :], scalar=stat[i][:, 32 + c : 33 + c], in1=gain[:, c, :], op0=MULT, op1=MULT
            )

        half = {}

        def gain_on_gpsimd(i):
            half[i] = soft.tile([P, T], F32, name="half", tag="half", bufs=2)
            nc.gpsimd.tensor_tensor(out=half[i][:], in0=expo[i][:, 1, :], in1=gain_sb[:], op=MULT)

        def factor_on_scalar(i):
            nc.scalar.activation(out=a_bf[i][:, 1, :], in_=half.pop(i)[:], func=COPY, scale=stat[i][:, 33:34])

        def turn_a(i, c):
            if c == 0:
                a_ps[i] = psum_w.tile([P, 2, 2, P], F32, name="w_ps")
            word = a_bf[i][:, c, :].bitcast(F32)
            for u in range(2):
                nc.tensor.transpose(a_ps[i][:, c, u, :], word[:, u * P : (u + 1) * P], ident[:])

        def copy_a(i, engine):
            a_grp[i] = soft.tile([P, C, P, PACK], BF16, name="a_grp", tag="a_grp", bufs=3, align_bytes=64)
            dst = a_grp[i][:].rearrange("p c n j -> p (c n j)").bitcast(F32).rearrange("p (c n u) -> p c n u", c=C, u=2)
            bank = a_ps.pop(i)[:].rearrange("p c u n -> p c n u")
            if engine == "VS":
                copy_on("S", dst[:, 0], bank[:, 0])
                copy_on("V", dst[:, 1], bank[:, 1])
            else:
                copy_on(engine, dst, bank)

        def quant_a(i, parts=1):
            cod = soft.tile([P, C * P], U32, name="a_cod", tag="a_cod", bufs=3, align_bytes=64)
            sca = soft.tile([P, C * P], U8, name="a_sca", tag="a_sca", bufs=3, align_bytes=64)
            src = a_grp.pop(i)[:].rearrange("p c n j -> p (c n j)")
            width = C * P // parts
            for n in range(parts):
                cols = slice(n * width, (n + 1) * width)
                nc.vector.quantize_mx(out=cod[:, cols].bitcast(FP8X4), scales=sca[:, cols], in_=src[:, PACK * n * width : PACK * (n + 1) * width])
            a_cod[i] = (cod, sca)

        def mix(i):
            h = i // PACK
            bank = psum_w.tile([P, EV], F32, name="w_ps")
            cod, sca = a_cod.pop(i)
            for c in range(C):
                cols = slice(c * P, (c + 1) * P)
                nc.tensor.matmul_mx(
                    out=bank[:],
                    lhsT=cod[:, cols].bitcast(FP8X4),
                    lhsT_scale=sca[:, cols],
                    rhs=vc[h, c][0][:].bitcast(FP8X4),
                    rhs_scale=vc[h, c][1][:],
                    start=(c == 0),
                    stop=(c == C - 1),
                )
            o_ps[i] = bank

        def copy_o(i, split=EV):
            h, t = divmod(i, PACK)
            if t == 0:
                o_sb[h] = res.tile([P, PACK, EV], F32, name="o_sb", tag="o_sb", bufs=3)
            bank = o_ps.pop(i)
            nc.scalar.copy(out=o_sb[h][:, t, :split], in_=bank[:, :split])
            if split < EV:
                nc.vector.tensor_copy(out=o_sb[h][:, t, split:], in_=bank[:, split:])

        def store_o(h, lo, hi):
            nc.sync.dma_start(out=out[h].rearrange("(p t) e -> p t e", t=PACK)[:, lo:hi, :], in_=o_sb[h][:, lo:hi, :])

        def weave_o(h, engine, lo=0, hi=EV):
            if h not in o_grp:
                o_grp[h] = res.tile([P, EV, PACK], BF16, name="o_grp", tag="o_grp", bufs=2, align_bytes=64)
            weave(o_grp[h], o_sb[h], engine, lo, hi)

        def planes(h, parts=1):
            cod, sca = quant(o_grp[h], "p_cod", 2, parts)
            width = EV // parts
            for a in range(parts):
                cols = slice(h * EV + a * width, h * EV + (a + 1) * width)
                here = slice(a * width, (a + 1) * width)
                nc.sync.dma_start(out=words[0, :, cols, :].rearrange("p m t -> p (m t)").bitcast(I32), in_=cod[:, here].bitcast(I32))
            cols = slice(h * EV, (h + 1) * EV)
            for b in range(4):
                nc.sync.dma_start(out=scales[0, 4 * b : 4 * b + 4, cols].bitcast(I32), in_=sca[32 * b : 32 * b + 4, :].bitcast(I32))

        OW = 384
        OFF = ()
        PIECES = ((1, 0, 0, 256), (1, 1, 256, 512), (0, 2, 0, 256), (0, 3, 256, 512))

        def prep(n):
            h, t = divmod(n + 2, PACK)
            return None if t == 3 or h + 1 >= H else ((h + 1,), (h + 1, 0), (h + 1, 1))[t]

        turn((0,), 0, "V")
        turn((0, 0), 0, "S")
        qc[0] = quant(grouped[0,], "q_cod", 2, 2, None, (0,))
        turn((0, 0), 1, "V")
        turn((0, 1), 0, "S")
        quant_k(0, 0)
        turn((0, 1), 1, "S")
        score(0, 0)
        score(1, 0)
        turn((0,), 1, "S")
        top(0, 0)
        quant_k(0, 1)
        top(1, 0)
        turn(prep(-2), 0, "S")
        score(0, 1)
        score(1, 1)
        make_gain()
        top(0, 1)
        shift(0)
        turn_only(prep(-2), 1)
        top(1, 1)
        expon(0, 0)
        expon(0, 1)
        shift(1)
        quant(grouped.pop((0,)), "q_cod", 2, 2, qc[0], (1,))
        copy_turn(prep(-2), 1, "S")
        weave_v(0, 0, "V", 0, 512)
        quant_q(1)
        turn(prep(-1), 0, "S")
        score(2, 0)
        score(2, 1)
        turn(prep(-1), 1, "S")

        for i in range(tiles - 1):
            h, t = divmod(i, PACK)
            more = h + 1 < H
            if i >= 2:
                quant_a(i - 2)
            if t == 0 and more:
                quant_k(h + 1, 0)
            if t == 1:
                quant_v(h, 0)
                if more:
                    quant_k(h + 1, 1)
            if t == 2:
                quant_v(h, 1)
            if t == 3 and h + 2 < H:
                quant_q(h + 2)
            recip(i)
            factor(i)
            offload = t in OFF
            if offload:
                gain_on_gpsimd(i)
            for part, t0, lo, hi in PIECES:
                if t0 == t and h + (part == 0) < H:
                    weave_v(h + (part == 0), part, "G", lo, hi)
            expon(i + 1, 0)
            expon(i + 1, 1)
            if i == 0:
                nc.scalar.copy(out=gain_sb[:], in_=gain[:, 1, :])
            key = prep(i)
            if key:
                turn_only(key, 0)
                turn_only(key, 1)
            if i >= 1:
                copy_a(i - 1, "S")
            if key:
                copy_turn(key, 0, "S")
                copy_turn(key, 1, "S")
            if i >= 2:
                mix(i - 2)
            if i + 3 < tiles:
                score(i + 3, 0)
                score(i + 3, 1)
            if i + 2 < tiles:
                top(i + 2, 0)
                top(i + 2, 1)
            weigh(i, 0)
            turn_a(i, 0)
            if offload:
                factor_on_scalar(i)
            else:
                weigh(i, 1)
            if i + 2 < tiles:
                shift(i + 2)
            turn_a(i, 1)
            if i >= 2:
                copy_o(i - 2)
                if (i - 2) % PACK == 3:
                    store_o((i - 2) // PACK, 0, 4)
                elif h == H - 1 and t >= 2:
                    store_o(h, t - 2, t - 1)
            if h > 0 and t == 1:
                weave_o(h - 1, "S", 0, OW)
            if h > 0 and t == 2:
                if OW < EV:
                    weave_o(h - 1, "V", OW, EV)
                planes(h - 1)

        z = tiles - 1
        quant_a(z - 2)
        recip(z)
        factor(z, nc.vector)
        copy_a(z - 1, "S")
        mix(z - 2)
        weigh(z, 0)
        turn_a(z, 0)
        copy_o(z - 2)
        store_o(H - 1, 1, 2)
        weigh(z, 1)
        turn_a(z, 1)
        quant_a(z - 1)
        copy_a(z, "VS")
        mix(z - 1)
        quant_a(z, 2)
        copy_o(z - 1)
        store_o(H - 1, 2, 3)
        mix(z)
        copy_o(z, EV // 2)
        store_o(H - 1, 3, 4)
        weave_o(H - 1, "V", 0, 256)
        weave_o(H - 1, "V", 256, 512)
        planes(H - 1, 2)
